import numpy as np, ml_dtypes
CORES = [23,119,17,113]
N = 4
NP, TK = 2, 128
def setup_inputs(rng):
    return {"x": rng.standard_normal((N, 128, TK), dtype=np.float32).astype(ml_dtypes.bfloat16), "w1": (rng.standard_normal((N, 128, 128), dtype=np.float32) / 8).astype(ml_dtypes.bfloat16), "w2": (rng.standard_normal((N, 128, NP * 128), dtype=np.float32) / 8).astype(ml_dtypes.bfloat16)}
def setup_inputs_big(rng):
    d = setup_inputs(rng)
    for k in ("x", "w1", "w2"): d[k] = (d[k].astype(np.float32) * 1024.0).astype(d[k].dtype)
    return d
def setup_inputs_small(rng):
    d = setup_inputs(rng)
    for k in ("x", "w1", "w2"): d[k] = (d[k].astype(np.float32) * (1 / 1024.0)).astype(d[k].dtype)
    return d
def setup_inputs_apart(rng):
    d = setup_inputs(rng)
    f = (10.0 ** rng.permutation(np.linspace(-1.5, 1.5, N))).astype(np.float32).reshape(N, 1, 1)
    for k in ("x", "w1", "w2"): d[k] = (d[k].astype(np.float32) * f).astype(d[k].dtype)
    return d
def reference(x, w1, w2):
    X, W1, W2 = x.astype(np.float64), w1.astype(np.float64), w2.astype(np.float64)
    h = [np.maximum(W1[p].T @ X[p], 0.0) for p in range(NP)]
    y = np.full((N, 128, TK), np.nan)
    for q in range(NP, N):
        y[q] = sum(W2[q][:, 128 * p:128 * p + 128].T @ h[p] for p in range(NP))
    return {"y": y.astype(ml_dtypes.bfloat16 if x.dtype != np.float64 else np.float64)}

@@ -1,0 +1,92 @@
+from concourse.bass import DstId, RemoteDMATransfer
+from concourse.mybir import AluOpType
+
+D = 128
+
+SCRATCH = {
+    "xs": ("sbuf", [D, D], "bfloat16"),
+    "w1s": ("sbuf", [D, D], "bfloat16"),
+    "zero": ("sbuf", [D, D], "float32"),
+    "hs": ("sbuf", [D, D], "bfloat16"),
+    "w2s": ("sbuf", [D, 2 * D], "bfloat16"),
+    "land0": ("sbuf", [D, D], "bfloat16"),
+    "land1": ("sbuf", [D, D], "bfloat16"),
+    "ys": ("sbuf", [D, D], "bfloat16"),
+    "acc": ("psum", [D, D], "float32"),
+}
+SEMAPHORES = ["loaded", "zeroed", "mm", "act", "sent", "arr0", "arr1", "stored"]
+
+K_FAR = 4
+K_NEAR = 4
+
+
+def _engines(mask):
+    return [e for e in range(mask.bit_length()) if (mask >> e) & 1]
+
+
+def _spread(pool, k):
+    step = len(pool) // k
+    m = 0
+    for e in pool[::step][:k]:
+        m |= 1 << e
+    return m
+
+
+def rank_program(g, core, T, topo):
+    rank = T.rank_of(core)
+    if rank is None:
+        return
+    n_p = T.w2.shape[1] // D
+    p_cores = list(T.cores[:n_p])
+    q_cores = list(T.cores[n_p:])
+
+    if rank < n_p:
+        g.sync.dma_start(T.xs[:], T.x[:]).then_inc(T.sem.loaded, 16)
+        g.scalar.dma_start(T.w1s[:], T.w1[:]).then_inc(T.sem.loaded, 16)
+        g.vector.memset(T.zero[:], 0.0).then_inc(T.sem.zeroed, 1)
+
+        g.tensor.wait_ge(T.sem.loaded, 32)
+        g.tensor.matmul(T.acc[:], T.w1s[:], T.xs[:], True, True).then_inc(T.sem.mm, 1)
+
+        g.vector.wait_ge(T.sem.zeroed, 1)
+        g.vector.wait_ge(T.sem.mm, 1)
+        g.vector.tensor_tensor(T.hs[:], T.acc[:], T.zero[:], AluOpType.max).then_inc(T.sem.act, 1)
+
+        far = [q for q in q_cores if topo.chip(q) != topo.chip(core)]
+        near = [q for q in q_cores if topo.chip(q) == topo.chip(core)]
+        off_chip = 0
+        for q in far:
+            off_chip |= topo.mask(core, q)
+        transfers, total = [], 0
+        for group, k in ((far, K_FAR), (near, K_NEAR)):
+            for i, q in enumerate(group):
+                open_to = topo.mask(core, q)
+                if group is near:
+                    open_to &= ~off_chip
+                pool = _engines(open_to)
+                share = len(pool) // len(group)
+                rid, pid, _ = topo.addr(q)
+                transfers.append(RemoteDMATransfer(
+                    dst_ids=[DstId(rid=rid, pnc=pid)],
+                    dma_engine_mask=_spread(pool[i * share:(i + 1) * share], k),
+                    remote_sem=T.sem["arr%d" % rank],
+                    src=T.hs[:], dst=T["land%d" % rank][:]))
+                total += k
+        g.wait_ge(T.sem.act, 1)
+        g.remote_dma_fused(transfers, local_sem=T.sem.sent)
+        g.wait_ge(T.sem.sent, total)
+        return
+
+    g.sync.dma_start(T.w2s[:], T.w2[:]).then_inc(T.sem.loaded, 16)
+    g.tensor.wait_ge(T.sem.loaded, 16)
+    order = sorted(range(n_p), key=lambda p: topo.chip(p_cores[p]) != topo.chip(core))
+    for j, p in enumerate(order):
+        k = K_NEAR if topo.chip(p_cores[p]) == topo.chip(core) else K_FAR
+        g.tensor.wait_ge(T.sem["arr%d" % p], k)
+        mm = g.tensor.matmul(T.acc[:], T.w2s[:, p * D:(p + 1) * D], T["land%d" % p][:], j == 0, j == n_p - 1)
+    mm.then_inc(T.sem.mm, 1)
+    g.vector.wait_ge(T.sem.mm, 1)
+    g.vector.tensor_copy(T.ys[:], T.acc[:]).then_inc(T.sem.act, 1)
+    g.sync.wait_ge(T.sem.act, 1)
+    g.sync.dma_start(T.y[:], T.ys[:]).then_inc(T.sem.stored, 16)
+    g.sync.wait_ge(T.sem.stored, 16)

@@ -1,35 +1,49 @@
-from concourse.bass import DstId, RemoteDMATransfer
 from concourse.mybir import AluOpType
 
 D = 128
+H = D // 2
+BANK = 512
 
 SCRATCH = {
-    "xs": ("sbuf", [D, D], "bfloat16"),
-    "w1s": ("sbuf", [D, D], "bfloat16"),
-    "zero": ("sbuf", [D, D], "float32"),
+    "xw": ("sbuf", [D, 2 * D], "bfloat16"),
+    "zero": ("sbuf", [D, H], "float32"),
     "hs": ("sbuf", [D, D], "bfloat16"),
     "w2s": ("sbuf", [D, 2 * D], "bfloat16"),
-    "land0": ("sbuf", [D, D], "bfloat16"),
-    "land1": ("sbuf", [D, D], "bfloat16"),
+    "land": ("sbuf", [D, D], "bfloat16"),
     "ys": ("sbuf", [D, D], "bfloat16"),
-    "acc": ("psum", [D, D], "float32"),
+    "hacc0": ("psum", [D, BANK], "float32"),
+    "hacc1": ("psum", [D, BANK], "float32"),
+    "acc0": ("psum", [D, BANK], "float32"),
+    "acc1": ("psum", [D, BANK], "float32"),
 }
-SEMAPHORES = ["loaded", "zeroed", "mm", "act", "sent", "arr0", "arr1", "stored"]
+SEMAPHORES = ["loaded", "zeroed", "hmm0", "hmm1", "act0", "act1", "sent", "raw", "arr", "mm0", "mm1",
+              "rounded0", "rounded1", "stored"]
 
 K_FAR = 4
-K_NEAR = 4
+K_RAW = 8
 
 
 def _engines(mask):
     return [e for e in range(mask.bit_length()) if (mask >> e) & 1]
 
 
-def _spread(pool, k):
-    step = len(pool) // k
+def _as_mask(engines):
     m = 0
-    for e in pool[::step][:k]:
+    for e in engines:
         m |= 1 << e
     return m
+
+
+def _make_h(g, T, sem, count):
+    g.vector.memset(T.zero[:], 0.0).then_inc(T.sem.zeroed, 1)
+    g.tensor.wait_ge(sem, count)
+    g.vector.wait_ge(T.sem.zeroed, 1)
+    for c in range(2):
+        cols = slice(c * H, (c + 1) * H)
+        g.tensor.matmul(T["hacc%d" % c][:, :H], T.xw[:, D:], T.xw[:, cols], True, True).then_inc(T.sem["hmm%d" % c], 1)
+        g.vector.wait_ge(T.sem["hmm%d" % c], 1)
+        g.vector.tensor_tensor(T.hs[:, cols], T["hacc%d" % c][:, :H], T.zero[:],
+                               AluOpType.max).then_inc(T.sem["act%d" % c], 1)
 
 
 def rank_program(g, core, T, topo):
@@ -41,52 +55,44 @@ def rank_program(g, core, T, topo):
     q_cores = list(T.cores[n_p:])
 
     if rank < n_p:
-        g.sync.dma_start(T.xs[:], T.x[:]).then_inc(T.sem.loaded, 16)
-        g.scalar.dma_start(T.w1s[:], T.w1[:]).then_inc(T.sem.loaded, 16)
-        g.vector.memset(T.zero[:], 0.0).then_inc(T.sem.zeroed, 1)
+        (near,) = [q for q in q_cores if topo.chip(q) == topo.chip(core)]
+        (far,) = [q for q in q_cores if topo.chip(q) != topo.chip(core)]
+        g.sync.dma_start(T.xw[:, :D], T.x[:]).then_inc(T.sem.loaded, 16)
+        g.scalar.dma_start(T.xw[:, D:], T.w1[:]).then_inc(T.sem.loaded, 16)
+        _make_h(g, T, T.sem.loaded, 32)
 
-        g.tensor.wait_ge(T.sem.loaded, 32)
-        g.tensor.matmul(T.acc[:], T.w1s[:], T.xs[:], True, True).then_inc(T.sem.mm, 1)
+        stay = _engines(topo.mask(core, near) & ~topo.mask(core, far))
+        rid, pid, _ = topo.addr(near)
+        g.wait_ge(T.sem.loaded, 32)
+        g.remote_dma(T.xw[:], T.xw[:], T.sem.raw, T.sem.sent, pid, rid, _as_mask(stay[:K_RAW]))
 
-        g.vector.wait_ge(T.sem.zeroed, 1)
-        g.vector.wait_ge(T.sem.mm, 1)
-        g.vector.tensor_tensor(T.hs[:], T.acc[:], T.zero[:], AluOpType.max).then_inc(T.sem.act, 1)
-
-        far = [q for q in q_cores if topo.chip(q) != topo.chip(core)]
-        near = [q for q in q_cores if topo.chip(q) == topo.chip(core)]
-        off_chip = 0
-        for q in far:
-            off_chip |= topo.mask(core, q)
-        transfers, total = [], 0
-        for group, k in ((far, K_FAR), (near, K_NEAR)):
-            for i, q in enumerate(group):
-                open_to = topo.mask(core, q)
-                if group is near:
-                    open_to &= ~off_chip
-                pool = _engines(open_to)
-                share = len(pool) // len(group)
-                rid, pid, _ = topo.addr(q)
-                transfers.append(RemoteDMATransfer(
-                    dst_ids=[DstId(rid=rid, pnc=pid)],
-                    dma_engine_mask=_spread(pool[i * share:(i + 1) * share], k),
-                    remote_sem=T.sem["arr%d" % rank],
-                    src=T.hs[:], dst=T["land%d" % rank][:]))
-                total += k
-        g.wait_ge(T.sem.act, 1)
-        g.remote_dma_fused(transfers, local_sem=T.sem.sent)
-        g.wait_ge(T.sem.sent, total)
+        leave = _engines(topo.mask(core, far))
+        rid, pid, _ = topo.addr(far)
+        g.wait_ge(T.sem.act0, 1)
+        g.wait_ge(T.sem.act1, 1)
+        g.remote_dma(T.land[:], T.hs[:], T.sem.arr, T.sem.sent, pid, rid,
+                     _as_mask(leave[::len(leave) // K_FAR][:K_FAR]))
+        g.wait_ge(T.sem.sent, K_RAW + K_FAR)
         return
 
+    (p_near,) = [p for p in range(n_p) if topo.chip(p_cores[p]) == topo.chip(core)]
+    (p_far,) = [p for p in range(n_p) if topo.chip(p_cores[p]) != topo.chip(core)]
+    w_near = T.w2s[:, p_near * D:(p_near + 1) * D]
+    w_far = T.w2s[:, p_far * D:(p_far + 1) * D]
     g.sync.dma_start(T.w2s[:], T.w2[:]).then_inc(T.sem.loaded, 16)
+    _make_h(g, T, T.sem.raw, K_RAW)
     g.tensor.wait_ge(T.sem.loaded, 16)
-    order = sorted(range(n_p), key=lambda p: topo.chip(p_cores[p]) != topo.chip(core))
-    for j, p in enumerate(order):
-        k = K_NEAR if topo.chip(p_cores[p]) == topo.chip(core) else K_FAR
-        g.tensor.wait_ge(T.sem["arr%d" % p], k)
-        mm = g.tensor.matmul(T.acc[:], T.w2s[:, p * D:(p + 1) * D], T["land%d" % p][:], j == 0, j == n_p - 1)
-    mm.then_inc(T.sem.mm, 1)
-    g.vector.wait_ge(T.sem.mm, 1)
-    g.vector.tensor_copy(T.ys[:], T.acc[:]).then_inc(T.sem.act, 1)
-    g.sync.wait_ge(T.sem.act, 1)
+    g.tensor.wait_ge(T.sem.act0, 1)
+    g.tensor.matmul(T.acc0[:, :H], w_near, T.hs[:, :H], True, False)
+    g.tensor.wait_ge(T.sem.arr, K_FAR)
+    g.tensor.matmul(T.acc0[:, :H], w_far, T.land[:, :H], False, True).then_inc(T.sem.mm0, 1)
+    g.tensor.matmul(T.acc1[:, :H], w_far, T.land[:, H:], True, False)
+    g.tensor.wait_ge(T.sem.act1, 1)
+    g.tensor.matmul(T.acc1[:, :H], w_near, T.hs[:, H:], False, True).then_inc(T.sem.mm1, 1)
+    for c in range(2):
+        g.vector.wait_ge(T.sem["mm%d" % c], 1)
+        g.vector.tensor_copy(T.ys[:, c * H:(c + 1) * H], T["acc%d" % c][:, :H]).then_inc(T.sem["rounded%d" % c], 1)
+    g.sync.wait_ge(T.sem.rounded0, 1)
+    g.sync.wait_ge(T.sem.rounded1, 1)
     g.sync.dma_start(T.y[:], T.ys[:]).then_inc(T.sem.stored, 16)
     g.sync.wait_ge(T.sem.stored, 16)

from concourse.mybir import AluOpType

D = 128
H = D // 2
BANK = 512

SCRATCH = {
    "xw": ("sbuf", [D, 2 * D], "bfloat16"),
    "zero": ("sbuf", [D, H], "float32"),
    "hs": ("sbuf", [D, D], "bfloat16"),
    "w2s": ("sbuf", [D, 2 * D], "bfloat16"),
    "land": ("sbuf", [D, D], "bfloat16"),
    "ys": ("sbuf", [D, D], "bfloat16"),
    "hacc0": ("psum", [D, BANK], "float32"),
    "hacc1": ("psum", [D, BANK], "float32"),
    "acc0": ("psum", [D, BANK], "float32"),
    "acc1": ("psum", [D, BANK], "float32"),
}
SEMAPHORES = ["loaded", "zeroed", "hmm0", "hmm1", "act0", "act1", "sent", "raw", "arr", "mm0", "mm1",
              "rounded0", "rounded1", "stored"]

K_FAR = 4
K_RAW = 8


def _engines(mask):
    return [e for e in range(mask.bit_length()) if (mask >> e) & 1]


def _as_mask(engines):
    m = 0
    for e in engines:
        m |= 1 << e
    return m


def _make_h(g, T, sem, count):
    g.vector.memset(T.zero[:], 0.0).then_inc(T.sem.zeroed, 1)
    g.tensor.wait_ge(sem, count)
    g.vector.wait_ge(T.sem.zeroed, 1)
    for c in range(2):
        cols = slice(c * H, (c + 1) * H)
        g.tensor.matmul(T["hacc%d" % c][:, :H], T.xw[:, D:], T.xw[:, cols], True, True).then_inc(T.sem["hmm%d" % c], 1)
        g.vector.wait_ge(T.sem["hmm%d" % c], 1)
        g.vector.tensor_tensor(T.hs[:, cols], T["hacc%d" % c][:, :H], T.zero[:],
                               AluOpType.max).then_inc(T.sem["act%d" % c], 1)


def rank_program(g, core, T, topo):
    rank = T.rank_of(core)
    if rank is None:
        return
    n_p = T.w2.shape[1] // D
    p_cores = list(T.cores[:n_p])
    q_cores = list(T.cores[n_p:])

    if rank < n_p:
        (near,) = [q for q in q_cores if topo.chip(q) == topo.chip(core)]
        (far,) = [q for q in q_cores if topo.chip(q) != topo.chip(core)]
        g.sync.dma_start(T.xw[:, :D], T.x[:]).then_inc(T.sem.loaded, 16)
        g.scalar.dma_start(T.xw[:, D:], T.w1[:]).then_inc(T.sem.loaded, 16)
        _make_h(g, T, T.sem.loaded, 32)

        stay = _engines(topo.mask(core, near) & ~topo.mask(core, far))
        rid, pid, _ = topo.addr(near)
        g.wait_ge(T.sem.loaded, 32)
        g.remote_dma(T.xw[:], T.xw[:], T.sem.raw, T.sem.sent, pid, rid, _as_mask(stay[:K_RAW]))

        leave = _engines(topo.mask(core, far))
        rid, pid, _ = topo.addr(far)
        g.wait_ge(T.sem.act0, 1)
        g.wait_ge(T.sem.act1, 1)
        g.remote_dma(T.land[:], T.hs[:], T.sem.arr, T.sem.sent, pid, rid,
                     _as_mask(leave[::len(leave) // K_FAR][:K_FAR]))
        g.wait_ge(T.sem.sent, K_RAW + K_FAR)
        return

    (p_near,) = [p for p in range(n_p) if topo.chip(p_cores[p]) == topo.chip(core)]
    (p_far,) = [p for p in range(n_p) if topo.chip(p_cores[p]) != topo.chip(core)]
    w_near = T.w2s[:, p_near * D:(p_near + 1) * D]
    w_far = T.w2s[:, p_far * D:(p_far + 1) * D]
    g.sync.dma_start(T.w2s[:], T.w2[:]).then_inc(T.sem.loaded, 16)
    _make_h(g, T, T.sem.raw, K_RAW)
    g.tensor.wait_ge(T.sem.loaded, 16)
    g.tensor.wait_ge(T.sem.act0, 1)
    g.tensor.matmul(T.acc0[:, :H], w_near, T.hs[:, :H], True, False)
    g.tensor.wait_ge(T.sem.arr, K_FAR)
    g.tensor.matmul(T.acc0[:, :H], w_far, T.land[:, :H], False, True).then_inc(T.sem.mm0, 1)
    g.tensor.matmul(T.acc1[:, :H], w_far, T.land[:, H:], True, False)
    g.tensor.wait_ge(T.sem.act1, 1)
    g.tensor.matmul(T.acc1[:, :H], w_near, T.hs[:, H:], False, True).then_inc(T.sem.mm1, 1)
    for c in range(2):
        g.vector.wait_ge(T.sem["mm%d" % c], 1)
        g.vector.tensor_copy(T.ys[:, c * H:(c + 1) * H], T["acc%d" % c][:, :H]).then_inc(T.sem["rounded%d" % c], 1)
    g.sync.wait_ge(T.sem.rounded0, 1)
    g.sync.wait_ge(T.sem.rounded1, 1)
    g.sync.dma_start(T.y[:], T.ys[:]).then_inc(T.sem.stored, 16)
    g.sync.wait_ge(T.sem.stored, 16)
